import numpy as np, ml_dtypes
CORES = [129,145,193,257,273,321,385,401,449]
N = 9
VB, TK = 1, 128
def setup_inputs(rng):
    h = rng.standard_normal((128, TK), dtype=np.float32) / 4; w = rng.standard_normal((N, 128, VB * 128), dtype=np.float32)
    a = 2 * np.pi * rng.random((TK)); s = 400 * rng.random((TK)) ** 1.5; h[0] = s * np.cos(a); h[1] = s * np.sin(a); h[2] = 150 * rng.standard_normal((TK)); w[:, 2, :] = 1 + w[:, 2, :] / 50
    a = (2 * np.pi * rng.random() + np.pi / 2 * (rng.permutation(N).reshape(N, 1, 1) + 0.5) / N - 0.5 + (np.arange(VB).reshape(1, VB, 1) + rng.random((N, VB, 128))) / VB).reshape(N, VB * 128); w[:, 0, :] = np.cos(a); w[:, 1, :] = np.sin(a)
    tgt = rng.integers(0, N * VB * 128, size=TK)
    oh = np.zeros((N * VB * 128, TK), np.float32); oh[tgt, np.arange(TK)] = 1.0
    oh = oh.reshape(N, VB, 128, TK).transpose(0, 2, 1, 3).reshape(N, 128, VB * TK)
    return {"h": np.broadcast_to(h, (N, 128, TK)).astype(ml_dtypes.bfloat16), "w": w.astype(ml_dtypes.bfloat16), "oh": oh.astype(ml_dtypes.bfloat16)}
def reference(h, w, oh):
    H, W, OH = h.astype(np.float64), w.astype(np.float64), oh.astype(np.float64)
    Z = np.concatenate([W[r].T @ H[r] for r in range(N)], axis=0)
    O = np.concatenate([OH[r][:, TK * b:TK * b + TK] for r in range(N) for b in range(VB)], axis=0)
    m = Z.max(axis=0)
    P = np.exp(Z - m); P = P / P.sum(axis=0)
    G = P - O
    d = sum(W[r] @ G[VB * 128 * r:VB * 128 * (r + 1)] for r in range(N)).astype(ml_dtypes.bfloat16)
    return {"d": np.broadcast_to(d, (N,) + d.shape)}

@@ -1,0 +1,211 @@
+from concourse.bass import DstId, RemoteDMATransfer
+from concourse.mybir import AluOpType, AxisListType, ActivationFunctionType
+
+NR = 9
+P = 128
+SLOT = 264
+V0, U0, SC, NC, MSG = 0, 128, 256, 257, 258
+
+SCRATCH = {
+    "h_sb": ("sbuf", [P, P], "bfloat16"),
+    "w_sb": ("sbuf", [P, P], "bfloat16"),
+    "oh_sb": ("sbuf", [P, P], "bfloat16"),
+    "ones": ("sbuf", [P, P], "bfloat16"),
+    "ident": ("sbuf", [P, P], "bfloat16"),
+    "zcol": ("sbuf", [P, 1], "float32"),
+    "wT1": ("sbuf", [P, 136], "bfloat16"),
+    "eT": ("sbuf", [P, P], "bfloat16"),
+    "e_sb": ("sbuf", [P, P], "bfloat16"),
+    "L": ("sbuf", [P, NR * SLOT], "bfloat16"),
+    "mn": ("sbuf", [P, 1], "float32"),
+    "a": ("sbuf", [P, NR], "float32"),
+    "as_": ("sbuf", [P, NR], "float32"),
+    "S": ("sbuf", [P, 1], "float32"),
+    "rS": ("sbuf", [P, 1], "float32"),
+    "an": ("sbuf", [P, NR], "float32"),
+    "diag": ("sbuf", [P, NR * P], "bfloat16"),
+    "dout": ("sbuf", [P, P], "bfloat16"),
+    "dland": ("dram", [P, P], "bfloat16"),
+    "wT_ps": ("psum", [P, 1024], "bfloat16"),
+    "e_ps": ("psum", [P, 1024], "bfloat16"),
+    "z_ps": ("psum", [P, 512], "float32"),
+    "u_ps": ("psum", [P, 512], "float32"),
+    "v_ps": ("psum", [P, 512], "float32"),
+    "d_ps": ("psum", [P, 512], "float32"),
+}
+SEMAPHORES = (["ld_w", "ld_h", "ld_oh", "ms_ones", "ms_z", "idn", "one", "z", "t1", "mx", "wtc", "ex", "t2", "ec",
+               "vm", "vc", "u", "uc", "sent", "mn", "aa", "asx", "ss", "rs", "an", "dmm", "dc", "fin", "st"]
+              + ["arr%d" % i for i in range(NR)] + ["dg%d" % i for i in range(NR)])
+
+
+def _bits(m):
+    return bin(m).count("1")
+
+
+def _plan(T, topo):
+    cores = list(T.cores)
+    centres = [c for c in cores
+               if all(o == c or (topo.may_write(o, c) and topo.may_write(c, o)) for o in cores)]
+    n = len(centres)
+
+    def group(x):
+        if x in centres:
+            return centres.index(x)
+        same = [i for i, c in enumerate(centres) if topo.chip(c) == topo.chip(x)]
+        return same[0] if same else cores.index(x) % n
+
+    def dests(x):
+        i = group(x)
+        return [centres[(i + j) % n] for j in range(n) if centres[(i + j) % n] != x]
+
+    def mask(x, ds):
+        m = topo.mask(x, ds[0])
+        for d in ds[1:]:
+            m &= topo.mask(x, d)
+        return m
+
+    return cores, centres, group, dests, mask
+
+
+def rank_program(g, core, T, topo):
+    rank = T.rank_of(core)
+    if rank is None:
+        return
+    cores, centres, group, dests, mask = _plan(T, topo)
+    n = len(centres)
+    sem = T.sem
+    pe, ve, se, sy = g.tensor, g.vector, g.scalar, g.sync
+    X, Alu, Act = AxisListType.X, AluOpType, ActivationFunctionType
+    L = T.L
+    o = rank * SLOT
+
+    sy.dma_start(T.w_sb[:], T.w[:]).then_inc(sem.ld_w, 16)
+    se.dma_start(T.h_sb[:], T.h[:]).then_inc(sem.ld_h, 16)
+    sy.dma_start(T.oh_sb[:], T.oh[:]).then_inc(sem.ld_oh, 16)
+    ve.memset(T.zcol[:], 0.0).then_inc(sem.ms_z, 1)
+    ve.memset(T.ones[:], 1.0).then_inc(sem.ms_ones, 1)
+    se.wait_ge(sem.ms_z, 1)
+    se.activation(T.wT1[:, P:P + 1], T.zcol[:], Act.Exp).then_inc(sem.one, 1)
+    g.wait_ge(sem.ms_ones, 1)
+    g.affine_select(T.ident[:], T.ones[:], [[-1, P]], Alu.is_equal, 0.0, 0, 1).then_inc(sem.idn, 1)
+
+    pe.wait_ge(sem.ld_w, 16)
+    pe.wait_ge(sem.ld_h, 16)
+    pe.matmul(T.z_ps[:, 0:P], T.h_sb[:], T.w_sb[:], True, True).then_inc(sem.z, 1)
+    pe.wait_ge(sem.idn, 1)
+    pe.transpose(T.wT_ps[:, 0:P], T.w_sb[:], T.ident[:]).then_inc(sem.t1, 1)
+
+    ve.wait_ge(sem.z, 1)
+    ve.tensor_reduce(L[:, o + NC:o + NC + 1], T.z_ps[:, 0:P], X, Alu.max, negate=True).then_inc(sem.mx, 1)
+    ve.wait_ge(sem.t1, 1)
+    ve.tensor_copy(T.wT1[:, 0:P], T.wT_ps[:, 0:P]).then_inc(sem.wtc, 1)
+
+    se.wait_ge(sem.z, 1)
+    se.wait_ge(sem.mx, 1)
+    se.activation(T.eT[:], T.z_ps[:, 0:P], Act.Exp, bias=L[:, o + NC:o + NC + 1]).then_inc(sem.ex, 1)
+
+    pe.wait_ge(sem.ex, 1)
+    pe.transpose(T.e_ps[:, 0:P], T.eT[:], T.ident[:]).then_inc(sem.t2, 1)
+    pe.wait_ge(sem.ld_oh, 16)
+    pe.wait_ge(sem.wtc, 1)
+    pe.matmul(T.v_ps[:, 0:P], T.oh_sb[:], T.wT1[:, 0:P], True, True).then_inc(sem.vm, 1)
+
+    ve.wait_ge(sem.t2, 1)
+    ve.tensor_copy(T.e_sb[:], T.e_ps[:, 0:P]).then_inc(sem.ec, 1)
+
+    pe.wait_ge(sem.ec, 1)
+    pe.wait_ge(sem.one, 1)
+    pe.matmul(T.u_ps[:, 0:P + 1], T.e_sb[:], T.wT1[:, 0:P + 1], True, True).then_inc(sem.u, 1)
+
+    se.wait_ge(sem.vm, 1)
+    se.activation(L[:, o + V0:o + V0 + P], T.v_ps[:, 0:P], Act.Identity, scale=-1.0).then_inc(sem.vc, 1)
+    ve.wait_ge(sem.u, 1)
+    ve.tensor_copy(L[:, o + U0:o + U0 + P + 1], T.u_ps[:, 0:P + 1]).then_inc(sem.uc, 1)
+
+    ds = dests(core)
+    m1 = mask(core, ds)
+    g.wait_ge(sem.mx, 1)
+    g.wait_ge(sem.vc, 1)
+    g.wait_ge(sem.uc, 1)
+    ids = []
+    for d in ds:
+        rid, pid = topo.addr(d, core)
+        ids.append(DstId(rid=rid, pnc=pid))
+    g.remote_dma_fused([RemoteDMATransfer(dst_ids=ids, dma_engine_mask=m1, remote_sem=sem["arr%d" % group(core)],
+                                          srcs=[L[:, o:o + MSG]], dsts=[L[:, o:o + MSG] for _ in ds], alu_op=0)],
+                       local_sem=sem.sent)
+    sent = _bits(m1)
+
+    if core not in centres:
+        c = centres[group(core)]
+        leaves = [x for x in cores if x not in centres and group(x) == group(core)]
+        sy.wait_ge(sem.fin, _bits(mask(c, leaves)))
+        sy.dma_start(T.d[:], T.dland[:]).then_inc(sem.st, 16)
+        sy.wait_ge(sem.st, 16)
+        g.wait_ge(sem.sent, sent)
+        return
+
+    k = group(core)
+    order = [(k - j) % n for j in range(n)]
+    cnt = {i: sum(_bits(mask(x, dests(x))) for x in cores if x != core and group(x) == i) for i in range(n)}
+    members = {i: [cores.index(x) for x in cores if x != core and group(x) == i] for i in range(n)}
+
+    pe.wait_ge(sem.vc, 1)
+    pe.matmul(T.d_ps[:, 0:P], L[:, o + V0:o + V0 + P], T.ident[:], True, False)
+    for i in order:
+        if cnt[i]:
+            pe.wait_ge(sem["arr%d" % i], cnt[i])
+        for r in members[i]:
+            pe.matmul(T.d_ps[:, 0:P], L[:, r * SLOT + V0:r * SLOT + V0 + P], T.ident[:], False, False)
+
+    for q in (ve, se):
+        for i in order:
+            if cnt[i]:
+                q.wait_ge(sem["arr%d" % i], cnt[i])
+        q.wait_ge(sem.mx, 1)
+        q.wait_ge(sem.uc, 1)
+        q.wait_ge(sem.idn, 1)
+    ve.tensor_reduce(T.mn[:], L[:, NC::SLOT], X, Alu.min).then_inc(sem.mn, 1)
+    se.wait_ge(sem.mn, 1)
+    se.activation(T.a[:], L[:, NC::SLOT], Act.Exp, bias=T.mn[:], scale=-1.0).then_inc(sem.aa, 1)
+    ve.wait_ge(sem.aa, 1)
+    ve.tensor_tensor(T.as_[:], T.a[:], L[:, SC::SLOT], Alu.mult).then_inc(sem.asx, 1)
+    ve.wait_ge(sem.asx, 1)
+    ve.tensor_reduce(T.S[:], T.as_[:], X, Alu.add).then_inc(sem.ss, 1)
+    ve.wait_ge(sem.ss, 1)
+    ve.reciprocal(T.rS[:], T.S[:]).then_inc(sem.rs, 1)
+    ve.wait_ge(sem.rs, 1)
+    ve.tensor_scalar(T.an[:], T.a[:], T.rS[:], None, Alu.mult).then_inc(sem.an, 1)
+    ve.wait_ge(sem.an, 1)
+    se.wait_ge(sem.an, 1)
+    for r in range(NR):
+        dg = T.diag[:, r * P:(r + 1) * P]
+        if r % 2 == 0:
+            ve.tensor_scalar(dg, T.ident[:], T.an[:, r:r + 1], None, Alu.mult).then_inc(sem["dg%d" % r], 1)
+        else:
+            se.activation(dg, T.ident[:], Act.Identity, scale=T.an[:, r:r + 1]).then_inc(sem["dg%d" % r], 1)
+    pe.wait_ge(sem.uc, 1)
+    for r in range(NR):
+        pe.wait_ge(sem["dg%d" % r], 1)
+        mm = pe.matmul(T.d_ps[:, 0:P], L[:, r * SLOT + U0:r * SLOT + U0 + P], T.diag[:, r * P:(r + 1) * P],
+                       False, r == NR - 1)
+    mm.then_inc(sem.dmm, 1)
+    ve.wait_ge(sem.dmm, 1)
+    ve.tensor_copy(T.dout[:], T.d_ps[:, 0:P]).then_inc(sem.dc, 1)
+
+    leaves = [x for x in cores if x not in centres and group(x) == k]
+    g.wait_ge(sem.dc, 1)
+    if leaves:
+        m2 = mask(core, leaves)
+        ids = []
+        for d in leaves:
+            rid, pid = topo.addr(d, core)
+            ids.append(DstId(rid=rid, pnc=pid))
+        g.remote_dma_fused([RemoteDMATransfer(dst_ids=ids, dma_engine_mask=m2, remote_sem=sem.fin,
+                                              srcs=[T.dout[:]], dsts=[T.dland[:] for _ in leaves], alu_op=0)],
+                           local_sem=sem.sent)
+        sent += _bits(m2)
+    sy.wait_ge(sem.dc, 1)
+    sy.dma_start(T.d[:], T.dout[:]).then_inc(sem.st, 16)
+    sy.wait_ge(sem.st, 16)
+    g.wait_ge(sem.sent, sent)

@@ -2,9 +2,15 @@ from concourse.bass import DstId, RemoteDMATransfer
 from concourse.mybir import AluOpType, AxisListType, ActivationFunctionType
 
 NR = 9
+NB = 3
 P = 128
-SLOT = 264
-V0, U0, SC, NC, MSG = 0, 128, 256, 257, 258
+WID = [48, 40, 40]
+BEG = [0, 48, 88]
+CW = 48
+C1 = CW + 1
+BW = 104
+U0, SC, V0, NC, MSG = 0, CW, C1, 2 * C1, 2 * C1 + 1
+OUT = NR * BW
 
 SCRATCH = {
     "h_sb": ("sbuf", [P, P], "bfloat16"),
@@ -12,11 +18,11 @@ SCRATCH = {
     "oh_sb": ("sbuf", [P, P], "bfloat16"),
     "ones": ("sbuf", [P, P], "bfloat16"),
     "ident": ("sbuf", [P, P], "bfloat16"),
-    "zcol": ("sbuf", [P, 1], "float32"),
-    "wT1": ("sbuf", [P, 136], "bfloat16"),
+    "zz": ("sbuf", [P, NB * C1], "bfloat16"),
+    "wTx": ("sbuf", [P, NB * C1], "bfloat16"),
     "eT": ("sbuf", [P, P], "bfloat16"),
     "e_sb": ("sbuf", [P, P], "bfloat16"),
-    "L": ("sbuf", [P, NR * SLOT], "bfloat16"),
+    "L": ("sbuf", [P, (NR + NB) * BW], "bfloat16"),
     "mn": ("sbuf", [P, 1], "float32"),
     "a": ("sbuf", [P, NR], "float32"),
     "as_": ("sbuf", [P, NR], "float32"),
@@ -24,18 +30,20 @@ SCRATCH = {
     "rS": ("sbuf", [P, 1], "float32"),
     "an": ("sbuf", [P, NR], "float32"),
     "diag": ("sbuf", [P, NR * P], "bfloat16"),
+    "dT": ("sbuf", [P, P], "bfloat16"),
     "dout": ("sbuf", [P, P], "bfloat16"),
-    "dland": ("dram", [P, P], "bfloat16"),
     "wT_ps": ("psum", [P, 1024], "bfloat16"),
     "e_ps": ("psum", [P, 1024], "bfloat16"),
+    "dF_ps": ("psum", [P, 1024], "bfloat16"),
     "z_ps": ("psum", [P, 512], "float32"),
     "u_ps": ("psum", [P, 512], "float32"),
     "v_ps": ("psum", [P, 512], "float32"),
-    "d_ps": ("psum", [P, 512], "float32"),
+    "dT_ps": ("psum", [P, 512], "float32"),
 }
-SEMAPHORES = (["ld_w", "ld_h", "ld_oh", "ms_ones", "ms_z", "idn", "one", "z", "t1", "mx", "wtc", "ex", "t2", "ec",
-               "vm", "vc", "u", "uc", "sent", "mn", "aa", "asx", "ss", "rs", "an", "dmm", "dc", "fin", "st"]
-              + ["arr%d" % i for i in range(NR)] + ["dg%d" % i for i in range(NR)])
+SEMAPHORES = (["ld_w", "ld_h", "ld_oh", "ms_ones", "ms_z", "idn", "one", "z", "t1", "mx", "ncc", "wtc", "ex", "t2",
+               "ec", "vm", "vc", "u", "uc", "sent", "mn", "aa", "asx", "ss", "rs", "an", "dmm", "dc", "fin", "tf",
+               "fc", "st"]
+              + ["arr%d" % i for i in range(NB)] + ["dg%d" % i for i in range(NR)])
 
 
 def _bits(m):
@@ -54,41 +62,49 @@ def _plan(T, topo):
         same = [i for i, c in enumerate(centres) if topo.chip(c) == topo.chip(x)]
         return same[0] if same else cores.index(x) % n
 
-    def dests(x):
-        i = group(x)
-        return [centres[(i + j) % n] for j in range(n) if centres[(i + j) % n] != x]
-
-    def mask(x, ds):
+    def common(x, ds):
         m = topo.mask(x, ds[0])
         for d in ds[1:]:
             m &= topo.mask(x, d)
         return m
 
-    return cores, centres, group, dests, mask
+    def hop1(x):
+        ks = [(group(x) + j) % n for j in range(n) if centres[(group(x) + j) % n] != x]
+        on = [b for b in range(16) if (common(x, [centres[k] for k in ks]) >> b) & 1]
+        per = 1
+        while per * 2 * len(ks) <= len(on):
+            per *= 2
+        return [(k, sum(1 << b for b in on[i * per:(i + 1) * per])) for i, k in enumerate(ks)]
+
+    return cores, centres, group, common, hop1
 
 
 def rank_program(g, core, T, topo):
     rank = T.rank_of(core)
     if rank is None:
         return
-    cores, centres, group, dests, mask = _plan(T, topo)
+    cores, centres, group, common, hop1 = _plan(T, topo)
     n = len(centres)
     sem = T.sem
     pe, ve, se, sy = g.tensor, g.vector, g.scalar, g.sync
     X, Alu, Act = AxisListType.X, AluOpType, ActivationFunctionType
     L = T.L
-    o = rank * SLOT
+    centre = core in centres
+
+    def blk(k):
+        return rank * BW if centre and centres[k] == core else OUT + k * BW
 
     sy.dma_start(T.w_sb[:], T.w[:]).then_inc(sem.ld_w, 16)
     se.dma_start(T.h_sb[:], T.h[:]).then_inc(sem.ld_h, 16)
     sy.dma_start(T.oh_sb[:], T.oh[:]).then_inc(sem.ld_oh, 16)
-    ve.memset(T.zcol[:], 0.0).then_inc(sem.ms_z, 1)
+    ve.memset(T.zz[:], 0.0).then_inc(sem.ms_z, 1)
     ve.memset(T.ones[:], 1.0).then_inc(sem.ms_ones, 1)
     se.wait_ge(sem.ms_z, 1)
-    se.activation(T.wT1[:, P:P + 1], T.zcol[:], Act.Exp).then_inc(sem.one, 1)
+    se.activation(T.wTx[:], T.zz[:], Act.Exp).then_inc(sem.one, 1)
     g.wait_ge(sem.ms_ones, 1)
     g.affine_select(T.ident[:], T.ones[:], [[-1, P]], Alu.is_equal, 0.0, 0, 1).then_inc(sem.idn, 1)
 
+    nc0 = L[:, blk(0) + NC:blk(0) + NC + 1]
     pe.wait_ge(sem.ld_w, 16)
     pe.wait_ge(sem.ld_h, 16)
     pe.matmul(T.z_ps[:, 0:P], T.h_sb[:], T.w_sb[:], True, True).then_inc(sem.z, 1)
@@ -96,116 +112,129 @@ def rank_program(g, core, T, topo):
     pe.transpose(T.wT_ps[:, 0:P], T.w_sb[:], T.ident[:]).then_inc(sem.t1, 1)
 
     ve.wait_ge(sem.z, 1)
-    ve.tensor_reduce(L[:, o + NC:o + NC + 1], T.z_ps[:, 0:P], X, Alu.max, negate=True).then_inc(sem.mx, 1)
+    ve.tensor_reduce(nc0, T.z_ps[:, 0:P], X, Alu.max, negate=True).then_inc(sem.mx, 1)
     ve.wait_ge(sem.t1, 1)
-    ve.tensor_copy(T.wT1[:, 0:P], T.wT_ps[:, 0:P]).then_inc(sem.wtc, 1)
+    ve.wait_ge(sem.one, 1)
+    for k in range(NB):
+        ve.tensor_copy(T.wTx[:, k * C1:k * C1 + WID[k]], T.wT_ps[:, BEG[k]:BEG[k] + WID[k]]).then_inc(sem.wtc, 1)
 
     se.wait_ge(sem.z, 1)
     se.wait_ge(sem.mx, 1)
-    se.activation(T.eT[:], T.z_ps[:, 0:P], Act.Exp, bias=L[:, o + NC:o + NC + 1]).then_inc(sem.ex, 1)
+    se.activation(T.eT[:], T.z_ps[:, 0:P], Act.Exp, bias=nc0).then_inc(sem.ex, 1)
+    for k in range(1, NB):
+        se.activation(L[:, blk(k) + NC:blk(k) + NC + 1], nc0, Act.Identity).then_inc(sem.ncc, 1)
 
     pe.wait_ge(sem.ex, 1)
     pe.transpose(T.e_ps[:, 0:P], T.eT[:], T.ident[:]).then_inc(sem.t2, 1)
     pe.wait_ge(sem.ld_oh, 16)
-    pe.wait_ge(sem.wtc, 1)
-    pe.matmul(T.v_ps[:, 0:P], T.oh_sb[:], T.wT1[:, 0:P], True, True).then_inc(sem.vm, 1)
+    pe.wait_ge(sem.wtc, NB)
+    pe.matmul(T.v_ps[:, 0:NB * C1], T.oh_sb[:], T.wTx[:], True, True).then_inc(sem.vm, 1)
 
     ve.wait_ge(sem.t2, 1)
     ve.tensor_copy(T.e_sb[:], T.e_ps[:, 0:P]).then_inc(sem.ec, 1)
 
     pe.wait_ge(sem.ec, 1)
-    pe.wait_ge(sem.one, 1)
-    pe.matmul(T.u_ps[:, 0:P + 1], T.e_sb[:], T.wT1[:, 0:P + 1], True, True).then_inc(sem.u, 1)
+    pe.matmul(T.u_ps[:, 0:NB * C1], T.e_sb[:], T.wTx[:], True, True).then_inc(sem.u, 1)
 
     se.wait_ge(sem.vm, 1)
-    se.activation(L[:, o + V0:o + V0 + P], T.v_ps[:, 0:P], Act.Identity, scale=-1.0).then_inc(sem.vc, 1)
+    for k in range(NB):
+        se.activation(L[:, blk(k) + V0:blk(k) + V0 + C1], T.v_ps[:, k * C1:(k + 1) * C1], Act.Identity,
+                      scale=-1.0).then_inc(sem.vc, 1)
     ve.wait_ge(sem.u, 1)
-    ve.tensor_copy(L[:, o + U0:o + U0 + P + 1], T.u_ps[:, 0:P + 1]).then_inc(sem.uc, 1)
+    for k in range(NB):
+        ve.tensor_copy(L[:, blk(k) + U0:blk(k) + U0 + C1], T.u_ps[:, k * C1:(k + 1) * C1]).then_inc(sem.uc, 1)
 
-    ds = dests(core)
-    m1 = mask(core, ds)
     g.wait_ge(sem.mx, 1)
-    g.wait_ge(sem.vc, 1)
-    g.wait_ge(sem.uc, 1)
-    ids = []
-    for d in ds:
-        rid, pid = topo.addr(d, core)
-        ids.append(DstId(rid=rid, pnc=pid))
-    g.remote_dma_fused([RemoteDMATransfer(dst_ids=ids, dma_engine_mask=m1, remote_sem=sem["arr%d" % group(core)],
-                                          srcs=[L[:, o:o + MSG]], dsts=[L[:, o:o + MSG] for _ in ds], alu_op=0)],
-                       local_sem=sem.sent)
-    sent = _bits(m1)
+    g.wait_ge(sem.ncc, NB - 1)
+    g.wait_ge(sem.vc, NB)
+    g.wait_ge(sem.uc, NB)
+    trs = []
+    sent = 0
+    for k, m in hop1(core):
+        rid, pid = topo.addr(centres[k], core)
+        trs.append(RemoteDMATransfer(dst_ids=[DstId(rid=rid, pnc=pid)], dma_engine_mask=m,
+                                     remote_sem=sem["arr%d" % group(core)],
+                                     src=L[:, blk(k):blk(k) + MSG], dst=L[:, rank * BW:rank * BW + MSG], alu_op=0))
+        sent += _bits(m)
+    g.remote_dma_fused(trs, local_sem=sem.sent)
 
-    if core not in centres:
-        c = centres[group(core)]
-        leaves = [x for x in cores if x not in centres and group(x) == group(core)]
-        sy.wait_ge(sem.fin, _bits(mask(c, leaves)))
-        sy.dma_start(T.d[:], T.dland[:]).then_inc(sem.st, 16)
-        sy.wait_ge(sem.st, 16)
-        g.wait_ge(sem.sent, sent)
-        return
+    def others(c):
+        i = group(c)
+        return [x for j in range(n) for x in cores if x != c and group(x) == (i + j) % n]
 
-    k = group(core)
-    order = [(k - j) % n for j in range(n)]
-    cnt = {i: sum(_bits(mask(x, dests(x))) for x in cores if x != core and group(x) == i) for i in range(n)}
-    members = {i: [cores.index(x) for x in cores if x != core and group(x) == i] for i in range(n)}
+    fin = sum(_bits(common(c, others(c))) for c in centres if c != core)
 
-    pe.wait_ge(sem.vc, 1)
-    pe.matmul(T.d_ps[:, 0:P], L[:, o + V0:o + V0 + P], T.ident[:], True, False)
-    for i in order:
-        if cnt[i]:
-            pe.wait_ge(sem["arr%d" % i], cnt[i])
-        for r in members[i]:
-            pe.matmul(T.d_ps[:, 0:P], L[:, r * SLOT + V0:r * SLOT + V0 + P], T.ident[:], False, False)
+    if centre:
+        k = group(core)
+        cnt = {i: sum(m for x in cores if x != core and group(x) == i
+                      for m in [_bits(mm) for kk, mm in hop1(x) if kk == k]) for i in range(n)}
+        members = {i: [cores.index(x) for x in cores if x != core and group(x) == i] for i in range(n)}
 
-    for q in (ve, se):
-        for i in order:
+        o = rank * BW
+        pe.wait_ge(sem.vc, NB)
+        pe.matmul(T.dT_ps[:, 0:C1], T.ident[:], L[:, o + V0:o + V0 + C1], True, False)
+        for i in range(n):
             if cnt[i]:
-                q.wait_ge(sem["arr%d" % i], cnt[i])
-        q.wait_ge(sem.mx, 1)
-        q.wait_ge(sem.uc, 1)
-        q.wait_ge(sem.idn, 1)
-    ve.tensor_reduce(T.mn[:], L[:, NC::SLOT], X, Alu.min).then_inc(sem.mn, 1)
-    se.wait_ge(sem.mn, 1)
-    se.activation(T.a[:], L[:, NC::SLOT], Act.Exp, bias=T.mn[:], scale=-1.0).then_inc(sem.aa, 1)
-    ve.wait_ge(sem.aa, 1)
-    ve.tensor_tensor(T.as_[:], T.a[:], L[:, SC::SLOT], Alu.mult).then_inc(sem.asx, 1)
-    ve.wait_ge(sem.asx, 1)
-    ve.tensor_reduce(T.S[:], T.as_[:], X, Alu.add).then_inc(sem.ss, 1)
-    ve.wait_ge(sem.ss, 1)
-    ve.reciprocal(T.rS[:], T.S[:]).then_inc(sem.rs, 1)
-    ve.wait_ge(sem.rs, 1)
-    ve.tensor_scalar(T.an[:], T.a[:], T.rS[:], None, Alu.mult).then_inc(sem.an, 1)
-    ve.wait_ge(sem.an, 1)
-    se.wait_ge(sem.an, 1)
-    for r in range(NR):
-        dg = T.diag[:, r * P:(r + 1) * P]
-        if r % 2 == 0:
-            ve.tensor_scalar(dg, T.ident[:], T.an[:, r:r + 1], None, Alu.mult).then_inc(sem["dg%d" % r], 1)
-        else:
-            se.activation(dg, T.ident[:], Act.Identity, scale=T.an[:, r:r + 1]).then_inc(sem["dg%d" % r], 1)
-    pe.wait_ge(sem.uc, 1)
-    for r in range(NR):
-        pe.wait_ge(sem["dg%d" % r], 1)
-        mm = pe.matmul(T.d_ps[:, 0:P], L[:, r * SLOT + U0:r * SLOT + U0 + P], T.diag[:, r * P:(r + 1) * P],
-                       False, r == NR - 1)
-    mm.then_inc(sem.dmm, 1)
-    ve.wait_ge(sem.dmm, 1)
-    ve.tensor_copy(T.dout[:], T.d_ps[:, 0:P]).then_inc(sem.dc, 1)
+                pe.wait_ge(sem["arr%d" % i], cnt[i])
+            for r in members[i]:
+                pe.matmul(T.dT_ps[:, 0:C1], T.ident[:], L[:, r * BW + V0:r * BW + V0 + C1], False, False)
 
-    leaves = [x for x in cores if x not in centres and group(x) == k]
-    g.wait_ge(sem.dc, 1)
-    if leaves:
-        m2 = mask(core, leaves)
+        for q in (ve, se):
+            for i in range(n):
+                if cnt[i]:
+                    q.wait_ge(sem["arr%d" % i], cnt[i])
+            q.wait_ge(sem.mx, 1)
+            q.wait_ge(sem.ncc, NB - 1)
+            q.wait_ge(sem.uc, NB)
+            q.wait_ge(sem.idn, 1)
+        ncs, scs = L[:, NC:OUT:BW], L[:, SC:OUT:BW]
+        ve.tensor_reduce(T.mn[:], ncs, X, Alu.min).then_inc(sem.mn, 1)
+        se.wait_ge(sem.mn, 1)
+        se.activation(T.a[:], ncs, Act.Exp, bias=T.mn[:], scale=-1.0).then_inc(sem.aa, 1)
+        ve.wait_ge(sem.aa, 1)
+        ve.tensor_tensor(T.as_[:], T.a[:], scs, Alu.mult).then_inc(sem.asx, 1)
+        ve.wait_ge(sem.asx, 1)
+        ve.tensor_reduce(T.S[:], T.as_[:], X, Alu.add).then_inc(sem.ss, 1)
+        ve.wait_ge(sem.ss, 1)
+        ve.reciprocal(T.rS[:], T.S[:]).then_inc(sem.rs, 1)
+        ve.wait_ge(sem.rs, 1)
+        ve.tensor_scalar(T.an[:], T.a[:], T.rS[:], None, Alu.mult).then_inc(sem.an, 1)
+        ve.wait_ge(sem.an, 1)
+        se.wait_ge(sem.an, 1)
+        for r in range(NR):
+            dg = T.diag[:, r * P:(r + 1) * P]
+            if r % 2 == 0:
+                ve.tensor_scalar(dg, T.ident[:], T.an[:, r:r + 1], None, Alu.mult).then_inc(sem["dg%d" % r], 1)
+            else:
+                se.activation(dg, T.ident[:], Act.Identity, scale=T.an[:, r:r + 1]).then_inc(sem["dg%d" % r], 1)
+        pe.wait_ge(sem.uc, NB)
+        for r in range(NR):
+            pe.wait_ge(sem["dg%d" % r], 1)
+            mm = pe.matmul(T.dT_ps[:, 0:C1], T.diag[:, r * P:(r + 1) * P], L[:, r * BW + U0:r * BW + U0 + C1],
+                           False, r == NR - 1)
+        mm.then_inc(sem.dmm, 1)
+        mine = T.dT[:, BEG[k]:BEG[k] + WID[k]]
+        ve.wait_ge(sem.dmm, 1)
+        ve.tensor_copy(mine, T.dT_ps[:, 0:WID[k]]).then_inc(sem.dc, 1)
+
+        ds = others(core)
+        m2 = common(core, ds)
         ids = []
-        for d in leaves:
+        for d in ds:
             rid, pid = topo.addr(d, core)
             ids.append(DstId(rid=rid, pnc=pid))
+        g.wait_ge(sem.dc, 1)
         g.remote_dma_fused([RemoteDMATransfer(dst_ids=ids, dma_engine_mask=m2, remote_sem=sem.fin,
-                                              srcs=[T.dout[:]], dsts=[T.dland[:] for _ in leaves], alu_op=0)],
+                                              srcs=[mine], dsts=[mine for _ in ds], alu_op=0)],
                            local_sem=sem.sent)
         sent += _bits(m2)
-    sy.wait_ge(sem.dc, 1)
+        pe.wait_ge(sem.dc, 1)
+
+    pe.wait_ge(sem.fin, fin)
+    pe.transpose(T.dF_ps[:, 0:P], T.dT[:], T.ident[:]).then_inc(sem.tf, 1)
+    ve.wait_ge(sem.tf, 1)
+    ve.tensor_copy(T.dout[:], T.dF_ps[:, 0:P]).then_inc(sem.fc, 1)
+    sy.wait_ge(sem.fc, 1)
     sy.dma_start(T.d[:], T.dout[:]).then_inc(sem.st, 16)
     sy.wait_ge(sem.st, 16)
     g.wait_ge(sem.sent, sent)

@@ -4,12 +4,12 @@ from concourse.mybir import AluOpType, AxisListType, ActivationFunctionType
 NR = 9
 NB = 3
 P = 128
-WID = [48, 40, 40]
-BEG = [0, 48, 88]
-CW = 48
+WID = [43, 43, 42]
+BEG = [0, 43, 86]
+CW = 43
 C1 = CW + 1
-BW = 104
-U0, SC, V0, NC, MSG = 0, CW, C1, 2 * C1, 2 * C1 + 1
+BW = 48
+SC, NC, UMSG = CW, C1, C1 + 1
 OUT = NR * BW
 
 SCRATCH = {
@@ -23,13 +23,15 @@ SCRATCH = {
     "eT": ("sbuf", [P, P], "bfloat16"),
     "e_sb": ("sbuf", [P, P], "bfloat16"),
     "L": ("sbuf", [P, (NR + NB) * BW], "bfloat16"),
+    "VL": ("sbuf", [P, (NR + NB) * BW], "bfloat16"),
+    "US": ("sbuf", [P, NR * BW], "bfloat16"),
     "mn": ("sbuf", [P, 1], "float32"),
     "a": ("sbuf", [P, NR], "float32"),
     "as_": ("sbuf", [P, NR], "float32"),
     "S": ("sbuf", [P, 1], "float32"),
     "rS": ("sbuf", [P, 1], "float32"),
     "an": ("sbuf", [P, NR], "float32"),
-    "diag": ("sbuf", [P, NR * P], "bfloat16"),
+    "stage": ("sbuf", [P, BW], "bfloat16"),
     "dT": ("sbuf", [P, P], "bfloat16"),
     "dout": ("sbuf", [P, P], "bfloat16"),
     "wT_ps": ("psum", [P, 1024], "bfloat16"),
@@ -41,9 +43,9 @@ SCRATCH = {
     "dT_ps": ("psum", [P, 512], "float32"),
 }
 SEMAPHORES = (["ld_w", "ld_h", "ld_oh", "ms_ones", "ms_z", "idn", "one", "z", "t1", "mx", "ncc", "wtc", "ex", "t2",
-               "ec", "vm", "vc", "u", "uc", "sent", "mn", "aa", "asx", "ss", "rs", "an", "dmm", "dc", "fin", "tf",
-               "fc", "st"]
-              + ["arr%d" % i for i in range(NB)] + ["dg%d" % i for i in range(NR)])
+               "ec", "vm", "vc", "u", "uc", "sent", "mn", "aa", "asx", "ss", "rs", "an", "dmm", "dc", "own", "fin",
+               "tf", "fc", "st"]
+              + ["au%d" % i for i in range(NB)] + ["av%d" % i for i in range(NB)] + ["sc%d" % i for i in range(NR)])
 
 
 def _bits(m):
@@ -88,7 +90,7 @@ def rank_program(g, core, T, topo):
     sem = T.sem
     pe, ve, se, sy = g.tensor, g.vector, g.scalar, g.sync
     X, Alu, Act = AxisListType.X, AluOpType, ActivationFunctionType
-    L = T.L
+    L, VL = T.L, T.VL
     centre = core in centres
 
     def blk(k):
@@ -138,25 +140,29 @@ def rank_program(g, core, T, topo):
 
     se.wait_ge(sem.vm, 1)
     for k in range(NB):
-        se.activation(L[:, blk(k) + V0:blk(k) + V0 + C1], T.v_ps[:, k * C1:(k + 1) * C1], Act.Identity,
+        se.activation(VL[:, blk(k):blk(k) + CW], T.v_ps[:, k * C1:k * C1 + CW], Act.Identity,
                       scale=-1.0).then_inc(sem.vc, 1)
     ve.wait_ge(sem.u, 1)
     for k in range(NB):
-        ve.tensor_copy(L[:, blk(k) + U0:blk(k) + U0 + C1], T.u_ps[:, k * C1:(k + 1) * C1]).then_inc(sem.uc, 1)
+        ve.tensor_copy(L[:, blk(k):blk(k) + C1], T.u_ps[:, k * C1:(k + 1) * C1]).then_inc(sem.uc, 1)
 
-    g.wait_ge(sem.mx, 1)
-    g.wait_ge(sem.ncc, NB - 1)
-    g.wait_ge(sem.vc, NB)
-    g.wait_ge(sem.uc, NB)
-    trs = []
     sent = 0
-    for k, m in hop1(core):
-        rid, pid = topo.addr(centres[k], core)
-        trs.append(RemoteDMATransfer(dst_ids=[DstId(rid=rid, pnc=pid)], dma_engine_mask=m,
-                                     remote_sem=sem["arr%d" % group(core)],
-                                     src=L[:, blk(k):blk(k) + MSG], dst=L[:, rank * BW:rank * BW + MSG], alu_op=0))
-        sent += _bits(m)
-    g.remote_dma_fused(trs, local_sem=sem.sent)
+    for buf, width, name in ((L, UMSG, "au"), (VL, CW, "av")):
+        if name == "au":
+            g.wait_ge(sem.mx, 1)
+            g.wait_ge(sem.ncc, NB - 1)
+            g.wait_ge(sem.uc, NB)
+        else:
+            g.wait_ge(sem.vc, NB)
+        trs = []
+        for k, m in hop1(core):
+            rid, pid = topo.addr(centres[k], core)
+            trs.append(RemoteDMATransfer(dst_ids=[DstId(rid=rid, pnc=pid)], dma_engine_mask=m,
+                                         remote_sem=sem["%s%d" % (name, group(core))],
+                                         src=buf[:, blk(k):blk(k) + width],
+                                         dst=buf[:, rank * BW:rank * BW + width], alu_op=0))
+            sent += _bits(m)
+        g.remote_dma_fused(trs, local_sem=sem.sent)
 
     def others(c):
         i = group(c)
@@ -169,24 +175,15 @@ def rank_program(g, core, T, topo):
         cnt = {i: sum(m for x in cores if x != core and group(x) == i
                       for m in [_bits(mm) for kk, mm in hop1(x) if kk == k]) for i in range(n)}
         members = {i: [cores.index(x) for x in cores if x != core and group(x) == i] for i in range(n)}
-
         o = rank * BW
-        pe.wait_ge(sem.vc, NB)
-        pe.matmul(T.dT_ps[:, 0:C1], T.ident[:], L[:, o + V0:o + V0 + C1], True, False)
-        for i in range(n):
-            if cnt[i]:
-                pe.wait_ge(sem["arr%d" % i], cnt[i])
-            for r in members[i]:
-                pe.matmul(T.dT_ps[:, 0:C1], T.ident[:], L[:, r * BW + V0:r * BW + V0 + C1], False, False)
 
         for q in (ve, se):
             for i in range(n):
                 if cnt[i]:
-                    q.wait_ge(sem["arr%d" % i], cnt[i])
+                    q.wait_ge(sem["au%d" % i], cnt[i])
             q.wait_ge(sem.mx, 1)
             q.wait_ge(sem.ncc, NB - 1)
             q.wait_ge(sem.uc, NB)
-            q.wait_ge(sem.idn, 1)
         ncs, scs = L[:, NC:OUT:BW], L[:, SC:OUT:BW]
         ve.tensor_reduce(T.mn[:], ncs, X, Alu.min).then_inc(sem.mn, 1)
         se.wait_ge(sem.mn, 1)
@@ -202,18 +199,28 @@ def rank_program(g, core, T, topo):
         ve.wait_ge(sem.an, 1)
         se.wait_ge(sem.an, 1)
         for r in range(NR):
-            dg = T.diag[:, r * P:(r + 1) * P]
+            us, ur = T.US[:, r * BW:r * BW + CW], L[:, r * BW:r * BW + CW]
             if r % 2 == 0:
-                ve.tensor_scalar(dg, T.ident[:], T.an[:, r:r + 1], None, Alu.mult).then_inc(sem["dg%d" % r], 1)
+                ve.tensor_scalar(us, ur, T.an[:, r:r + 1], None, Alu.mult).then_inc(sem["sc%d" % r], 1)
             else:
-                se.activation(dg, T.ident[:], Act.Identity, scale=T.an[:, r:r + 1]).then_inc(sem["dg%d" % r], 1)
-        pe.wait_ge(sem.uc, NB)
+                se.activation(us, ur, Act.Identity, scale=T.an[:, r:r + 1]).then_inc(sem["sc%d" % r], 1)
+
+        acc = T.dT_ps[:, 0:CW]
+        pe.wait_ge(sem.vc, NB)
+        pe.matmul(acc, T.ident[:], VL[:, o:o + CW], True, False)
         for r in range(NR):
-            pe.wait_ge(sem["dg%d" % r], 1)
-            mm = pe.matmul(T.dT_ps[:, 0:C1], T.diag[:, r * P:(r + 1) * P], L[:, r * BW + U0:r * BW + U0 + C1],
-                           False, r == NR - 1)
+            pe.wait_ge(sem["sc%d" % r], 1)
+            pe.matmul(acc, T.ident[:], T.US[:, r * BW:r * BW + CW], False, False)
+        rest = [(i, r) for i in range(n) for r in members[i]]
+        seen = []
+        for i, r in rest:
+            if i not in seen:
+                seen.append(i)
+                pe.wait_ge(sem["av%d" % i], cnt[i])
+            mm = pe.matmul(acc, T.ident[:], VL[:, r * BW:r * BW + CW], False, (i, r) == rest[-1])
         mm.then_inc(sem.dmm, 1)
-        mine = T.dT[:, BEG[k]:BEG[k] + WID[k]]
+        mine = T.stage[:, 0:WID[k]]
+        there = T.dT[:, BEG[k]:BEG[k] + WID[k]]
         ve.wait_ge(sem.dmm, 1)
         ve.tensor_copy(mine, T.dT_ps[:, 0:WID[k]]).then_inc(sem.dc, 1)
 
@@ -225,10 +232,12 @@ def rank_program(g, core, T, topo):
             ids.append(DstId(rid=rid, pnc=pid))
         g.wait_ge(sem.dc, 1)
         g.remote_dma_fused([RemoteDMATransfer(dst_ids=ids, dma_engine_mask=m2, remote_sem=sem.fin,
-                                              srcs=[mine], dsts=[mine for _ in ds], alu_op=0)],
+                                              srcs=[mine], dsts=[there for _ in ds], alu_op=0)],
                            local_sem=sem.sent)
         sent += _bits(m2)
-        pe.wait_ge(sem.dc, 1)
+        sy.wait_ge(sem.dc, 1)
+        sy.dma_start(there, mine).then_inc(sem.own, 16)
+        pe.wait_ge(sem.own, 16)
 
     pe.wait_ge(sem.fin, fin)
     pe.transpose(T.dF_ps[:, 0:P], T.dT[:], T.ident[:]).then_inc(sem.tf, 1)

from concourse.bass import DstId, RemoteDMATransfer
from concourse.mybir import AluOpType, AxisListType, ActivationFunctionType

NR = 9
NB = 3
P = 128
WID = [43, 43, 42]
BEG = [0, 43, 86]
CW = 43
C1 = CW + 1
BW = 48
SC, NC, UMSG = CW, C1, C1 + 1
OUT = NR * BW

SCRATCH = {
    "h_sb": ("sbuf", [P, P], "bfloat16"),
    "w_sb": ("sbuf", [P, P], "bfloat16"),
    "oh_sb": ("sbuf", [P, P], "bfloat16"),
    "ones": ("sbuf", [P, P], "bfloat16"),
    "ident": ("sbuf", [P, P], "bfloat16"),
    "zz": ("sbuf", [P, NB * C1], "bfloat16"),
    "wTx": ("sbuf", [P, NB * C1], "bfloat16"),
    "eT": ("sbuf", [P, P], "bfloat16"),
    "e_sb": ("sbuf", [P, P], "bfloat16"),
    "L": ("sbuf", [P, (NR + NB) * BW], "bfloat16"),
    "VL": ("sbuf", [P, (NR + NB) * BW], "bfloat16"),
    "US": ("sbuf", [P, NR * BW], "bfloat16"),
    "mn": ("sbuf", [P, 1], "float32"),
    "a": ("sbuf", [P, NR], "float32"),
    "as_": ("sbuf", [P, NR], "float32"),
    "S": ("sbuf", [P, 1], "float32"),
    "rS": ("sbuf", [P, 1], "float32"),
    "an": ("sbuf", [P, NR], "float32"),
    "stage": ("sbuf", [P, BW], "bfloat16"),
    "dT": ("sbuf", [P, P], "bfloat16"),
    "dout": ("sbuf", [P, P], "bfloat16"),
    "wT_ps": ("psum", [P, 1024], "bfloat16"),
    "e_ps": ("psum", [P, 1024], "bfloat16"),
    "dF_ps": ("psum", [P, 1024], "bfloat16"),
    "z_ps": ("psum", [P, 512], "float32"),
    "u_ps": ("psum", [P, 512], "float32"),
    "v_ps": ("psum", [P, 512], "float32"),
    "dT_ps": ("psum", [P, 512], "float32"),
}
SEMAPHORES = (["ld_w", "ld_h", "ld_oh", "ms_ones", "ms_z", "idn", "one", "z", "t1", "mx", "ncc", "wtc", "ex", "t2",
               "ec", "vm", "vc", "u", "uc", "sent", "mn", "aa", "asx", "ss", "rs", "an", "dmm", "dc", "own", "fin",
               "tf", "fc", "st"]
              + ["au%d" % i for i in range(NB)] + ["av%d" % i for i in range(NB)] + ["sc%d" % i for i in range(NR)])


def _bits(m):
    return bin(m).count("1")


def _plan(T, topo):
    cores = list(T.cores)
    centres = [c for c in cores
               if all(o == c or (topo.may_write(o, c) and topo.may_write(c, o)) for o in cores)]
    n = len(centres)

    def group(x):
        if x in centres:
            return centres.index(x)
        same = [i for i, c in enumerate(centres) if topo.chip(c) == topo.chip(x)]
        return same[0] if same else cores.index(x) % n

    def common(x, ds):
        m = topo.mask(x, ds[0])
        for d in ds[1:]:
            m &= topo.mask(x, d)
        return m

    def hop1(x):
        ks = [(group(x) + j) % n for j in range(n) if centres[(group(x) + j) % n] != x]
        on = [b for b in range(16) if (common(x, [centres[k] for k in ks]) >> b) & 1]
        per = 1
        while per * 2 * len(ks) <= len(on):
            per *= 2
        return [(k, sum(1 << b for b in on[i * per:(i + 1) * per])) for i, k in enumerate(ks)]

    return cores, centres, group, common, hop1


def rank_program(g, core, T, topo):
    rank = T.rank_of(core)
    if rank is None:
        return
    cores, centres, group, common, hop1 = _plan(T, topo)
    n = len(centres)
    sem = T.sem
    pe, ve, se, sy = g.tensor, g.vector, g.scalar, g.sync
    X, Alu, Act = AxisListType.X, AluOpType, ActivationFunctionType
    L, VL = T.L, T.VL
    centre = core in centres

    def blk(k):
        return rank * BW if centre and centres[k] == core else OUT + k * BW

    sy.dma_start(T.w_sb[:], T.w[:]).then_inc(sem.ld_w, 16)
    se.dma_start(T.h_sb[:], T.h[:]).then_inc(sem.ld_h, 16)
    sy.dma_start(T.oh_sb[:], T.oh[:]).then_inc(sem.ld_oh, 16)
    ve.memset(T.zz[:], 0.0).then_inc(sem.ms_z, 1)
    ve.memset(T.ones[:], 1.0).then_inc(sem.ms_ones, 1)
    se.wait_ge(sem.ms_z, 1)
    se.activation(T.wTx[:], T.zz[:], Act.Exp).then_inc(sem.one, 1)
    g.wait_ge(sem.ms_ones, 1)
    g.affine_select(T.ident[:], T.ones[:], [[-1, P]], Alu.is_equal, 0.0, 0, 1).then_inc(sem.idn, 1)

    nc0 = L[:, blk(0) + NC:blk(0) + NC + 1]
    pe.wait_ge(sem.ld_w, 16)
    pe.wait_ge(sem.ld_h, 16)
    pe.matmul(T.z_ps[:, 0:P], T.h_sb[:], T.w_sb[:], True, True).then_inc(sem.z, 1)
    pe.wait_ge(sem.idn, 1)
    pe.transpose(T.wT_ps[:, 0:P], T.w_sb[:], T.ident[:]).then_inc(sem.t1, 1)

    ve.wait_ge(sem.z, 1)
    ve.tensor_reduce(nc0, T.z_ps[:, 0:P], X, Alu.max, negate=True).then_inc(sem.mx, 1)
    ve.wait_ge(sem.t1, 1)
    ve.wait_ge(sem.one, 1)
    for k in range(NB):
        ve.tensor_copy(T.wTx[:, k * C1:k * C1 + WID[k]], T.wT_ps[:, BEG[k]:BEG[k] + WID[k]]).then_inc(sem.wtc, 1)

    se.wait_ge(sem.z, 1)
    se.wait_ge(sem.mx, 1)
    se.activation(T.eT[:], T.z_ps[:, 0:P], Act.Exp, bias=nc0).then_inc(sem.ex, 1)
    for k in range(1, NB):
        se.activation(L[:, blk(k) + NC:blk(k) + NC + 1], nc0, Act.Identity).then_inc(sem.ncc, 1)

    pe.wait_ge(sem.ex, 1)
    pe.transpose(T.e_ps[:, 0:P], T.eT[:], T.ident[:]).then_inc(sem.t2, 1)
    pe.wait_ge(sem.ld_oh, 16)
    pe.wait_ge(sem.wtc, NB)
    pe.matmul(T.v_ps[:, 0:NB * C1], T.oh_sb[:], T.wTx[:], True, True).then_inc(sem.vm, 1)

    ve.wait_ge(sem.t2, 1)
    ve.tensor_copy(T.e_sb[:], T.e_ps[:, 0:P]).then_inc(sem.ec, 1)

    pe.wait_ge(sem.ec, 1)
    pe.matmul(T.u_ps[:, 0:NB * C1], T.e_sb[:], T.wTx[:], True, True).then_inc(sem.u, 1)

    se.wait_ge(sem.vm, 1)
    for k in range(NB):
        se.activation(VL[:, blk(k):blk(k) + CW], T.v_ps[:, k * C1:k * C1 + CW], Act.Identity,
                      scale=-1.0).then_inc(sem.vc, 1)
    ve.wait_ge(sem.u, 1)
    for k in range(NB):
        ve.tensor_copy(L[:, blk(k):blk(k) + C1], T.u_ps[:, k * C1:(k + 1) * C1]).then_inc(sem.uc, 1)

    sent = 0
    for buf, width, name in ((L, UMSG, "au"), (VL, CW, "av")):
        if name == "au":
            g.wait_ge(sem.mx, 1)
            g.wait_ge(sem.ncc, NB - 1)
            g.wait_ge(sem.uc, NB)
        else:
            g.wait_ge(sem.vc, NB)
        trs = []
        for k, m in hop1(core):
            rid, pid = topo.addr(centres[k], core)
            trs.append(RemoteDMATransfer(dst_ids=[DstId(rid=rid, pnc=pid)], dma_engine_mask=m,
                                         remote_sem=sem["%s%d" % (name, group(core))],
                                         src=buf[:, blk(k):blk(k) + width],
                                         dst=buf[:, rank * BW:rank * BW + width], alu_op=0))
            sent += _bits(m)
        g.remote_dma_fused(trs, local_sem=sem.sent)

    def others(c):
        i = group(c)
        return [x for j in range(n) for x in cores if x != c and group(x) == (i + j) % n]

    fin = sum(_bits(common(c, others(c))) for c in centres if c != core)

    if centre:
        k = group(core)
        cnt = {i: sum(m for x in cores if x != core and group(x) == i
                      for m in [_bits(mm) for kk, mm in hop1(x) if kk == k]) for i in range(n)}
        members = {i: [cores.index(x) for x in cores if x != core and group(x) == i] for i in range(n)}
        o = rank * BW

        for q in (ve, se):
            for i in range(n):
                if cnt[i]:
                    q.wait_ge(sem["au%d" % i], cnt[i])
            q.wait_ge(sem.mx, 1)
            q.wait_ge(sem.ncc, NB - 1)
            q.wait_ge(sem.uc, NB)
        ncs, scs = L[:, NC:OUT:BW], L[:, SC:OUT:BW]
        ve.tensor_reduce(T.mn[:], ncs, X, Alu.min).then_inc(sem.mn, 1)
        se.wait_ge(sem.mn, 1)
        se.activation(T.a[:], ncs, Act.Exp, bias=T.mn[:], scale=-1.0).then_inc(sem.aa, 1)
        ve.wait_ge(sem.aa, 1)
        ve.tensor_tensor(T.as_[:], T.a[:], scs, Alu.mult).then_inc(sem.asx, 1)
        ve.wait_ge(sem.asx, 1)
        ve.tensor_reduce(T.S[:], T.as_[:], X, Alu.add).then_inc(sem.ss, 1)
        ve.wait_ge(sem.ss, 1)
        ve.reciprocal(T.rS[:], T.S[:]).then_inc(sem.rs, 1)
        ve.wait_ge(sem.rs, 1)
        ve.tensor_scalar(T.an[:], T.a[:], T.rS[:], None, Alu.mult).then_inc(sem.an, 1)
        ve.wait_ge(sem.an, 1)
        se.wait_ge(sem.an, 1)
        for r in range(NR):
            us, ur = T.US[:, r * BW:r * BW + CW], L[:, r * BW:r * BW + CW]
            if r % 2 == 0:
                ve.tensor_scalar(us, ur, T.an[:, r:r + 1], None, Alu.mult).then_inc(sem["sc%d" % r], 1)
            else:
                se.activation(us, ur, Act.Identity, scale=T.an[:, r:r + 1]).then_inc(sem["sc%d" % r], 1)

        acc = T.dT_ps[:, 0:CW]
        pe.wait_ge(sem.vc, NB)
        pe.matmul(acc, T.ident[:], VL[:, o:o + CW], True, False)
        for r in range(NR):
            pe.wait_ge(sem["sc%d" % r], 1)
            pe.matmul(acc, T.ident[:], T.US[:, r * BW:r * BW + CW], False, False)
        rest = [(i, r) for i in range(n) for r in members[i]]
        seen = []
        for i, r in rest:
            if i not in seen:
                seen.append(i)
                pe.wait_ge(sem["av%d" % i], cnt[i])
            mm = pe.matmul(acc, T.ident[:], VL[:, r * BW:r * BW + CW], False, (i, r) == rest[-1])
        mm.then_inc(sem.dmm, 1)
        mine = T.stage[:, 0:WID[k]]
        there = T.dT[:, BEG[k]:BEG[k] + WID[k]]
        ve.wait_ge(sem.dmm, 1)
        ve.tensor_copy(mine, T.dT_ps[:, 0:WID[k]]).then_inc(sem.dc, 1)

        ds = others(core)
        m2 = common(core, ds)
        ids = []
        for d in ds:
            rid, pid = topo.addr(d, core)
            ids.append(DstId(rid=rid, pnc=pid))
        g.wait_ge(sem.dc, 1)
        g.remote_dma_fused([RemoteDMATransfer(dst_ids=ids, dma_engine_mask=m2, remote_sem=sem.fin,
                                              srcs=[mine], dsts=[there for _ in ds], alu_op=0)],
                           local_sem=sem.sent)
        sent += _bits(m2)
        sy.wait_ge(sem.dc, 1)
        sy.dma_start(there, mine).then_inc(sem.own, 16)
        pe.wait_ge(sem.own, 16)

    pe.wait_ge(sem.fin, fin)
    pe.transpose(T.dF_ps[:, 0:P], T.dT[:], T.ident[:]).then_inc(sem.tf, 1)
    ve.wait_ge(sem.tf, 1)
    ve.tensor_copy(T.dout[:], T.dF_ps[:, 0:P]).then_inc(sem.fc, 1)
    sy.wait_ge(sem.fc, 1)
    sy.dma_start(T.d[:], T.dout[:]).then_inc(sem.st, 16)
    sy.wait_ge(sem.st, 16)
    g.wait_ge(sem.sent, sent)
